import numpy as np
import ml_dtypes


def mxq(x, axis, fmt="e4m3"):
    dtype, down = {"e4m3": (ml_dtypes.float8_e4m3fn, 7), "e5m2": (ml_dtypes.float8_e5m2, 14)}[fmt]
    v = np.moveaxis(np.asarray(x, np.float32).astype(ml_dtypes.bfloat16).astype(np.float64), axis, -1)
    blocks = v.reshape(v.shape[:-1] + (-1, 32))
    amax = np.abs(blocks).max(-1, keepdims=True)
    byte = np.maximum(np.where(amax > 0, np.frexp(amax)[1] - 1 + 127, 0) - down, 1)
    scale = np.exp2(byte - 127.0)
    codes = (blocks / scale).astype(np.float32).astype(dtype).astype(np.float64)
    return np.moveaxis((codes * scale).reshape(v.shape), -1, axis)


WIDE = False


def mx_kscale(k):
    if not WIDE:
        return np.ones(k)
    levels = np.array([10, -10, 5, -5, 0])
    if k % 512:
        return np.exp2(np.random.permutation(np.resize(levels, k // 32))).repeat(32)
    a = np.empty((k // 512, 16))
    for p in range(k // 512):
        a[p, :8] = np.random.permutation(np.resize(levels, 8))
        for g in range(8):
            far = levels[np.abs(levels - a[p, g]) >= 10]
            a[p, g + 8] = far[np.random.randint(len(far))]
    return np.exp2(a.ravel()).repeat(32)


def f64(x):
    return np.asarray(x).astype(np.float64)


def striped8(idx):
    return np.concatenate([v.reshape(-1, 16).T for v in idx]).astype(np.uint16)


def unstriped8(offs):
    return np.stack([offs[16 * g:16 * g + 16].T.reshape(-1) for g in range(8)]).astype(np.int64)


E2M1 = np.array([0.0, 0.5, 1.0, 1.5, 2.0, 3.0, 4.0, 6.0, -0.0, -0.5, -1.0, -1.5, -2.0, -3.0, -4.0, -6.0])


def pack_weight(w, fmt):
    k, n = w.shape
    w = f64(np.asarray(w, np.float32).astype(ml_dtypes.bfloat16)).reshape(k // 32, 32, n)
    amax = np.abs(w).max(1)
    if fmt == "e4m3":
        byte = np.frexp(amax)[1] - 1 + 127 - 7
    else:
        mant, ex = np.frexp(amax / 6.0)
        byte = np.where(mant > 0.5, ex, ex - 1) + 127
    byte = np.clip(np.where(amax > 0, byte, 1), 1, 254)
    scaled = (w * np.exp2(127.0 - byte)[:, None, :]).reshape(k, n).astype(np.float32)
    by_word = np.ascontiguousarray(scaled.reshape(k // 512, 128, 4, n).transpose(0, 1, 3, 2))
    if fmt == "e4m3":
        words = by_word.astype(ml_dtypes.float8_e4m3fn).view(np.uint8)
    else:
        c = by_word.astype(ml_dtypes.float4_e2m1fn).view(np.uint8) & 0xF
        words = (c[..., 0::2] | (c[..., 1::2] << 4)).reshape(k // 512, 128, 2 * n)
    return np.ascontiguousarray(words), np.ascontiguousarray(byte.astype(np.uint8).reshape(k // 512, 16, n))


def unpack_weight(words, scales, fmt):
    g, _, n = scales.shape
    words = np.ascontiguousarray(words).reshape(g, 128, n, -1)
    if fmt == "e4m3":
        vals = words.view(ml_dtypes.float8_e4m3fn).astype(np.float64)
    else:
        nib = np.empty((g, 128, n, 4), np.uint8)
        nib[..., 0::2] = words & 0xF
        nib[..., 1::2] = words >> 4
        vals = E2M1[nib]
    vals = vals * np.repeat(np.exp2(scales.astype(np.float64) - 127.0), 8, axis=1)[..., None]
    return vals.transpose(0, 1, 3, 2).reshape(g * 512, n)


K, M, T, S = 1536, 512, 1024, 512


def setup_inputs():
    n = np.random.standard_normal
    s = mx_kscale(K)[:, None]
    p_w = pack_weight(n((K, M)) / np.sqrt(K) / s, "e2m1")
    return {
        "xT": (n((K, T)) * s).astype(np.float32),
        "w_words": p_w[0],
        "w_scales": p_w[1],
        "wgt": np.repeat(np.random.uniform(0.5, 2.0, (8, S)), 16, axis=0).astype(np.float32),
        "b": (0.3 * n(512)).astype(np.float32),
        "offs": striped8(np.stack([np.random.permutation(T)[:S] for _ in range(8)])),
    }


def reference(xT, w_words, w_scales, wgt, b, offs):
    idx = unstriped8(offs)
    group = np.arange(K) % 512 // 64
    xg = f64(wgt)[np.arange(K) // 4 % 128] * f64(xT)[np.arange(K)[:, None], idx[group]]
    xT_ = mxq(xg, 0, "e4m3")
    w_ = unpack_weight(w_words, w_scales, "e2m1")
    y = w_.T @ xT_
    return y + f64(b)[:, None]

@@ -1,0 +1,183 @@
+from contextlib import ExitStack
+
+import concourse.mybir as mybir
+from concourse.masks import make_identity
+
+K, M, T, S = 1536, 512, 1024, 512
+FLOPS = 2 * K * M * S
+
+F32 = mybir.dt.float32
+BF16 = mybir.dt.bfloat16
+I32 = mybir.dt.int32
+U32 = mybir.dt.uint32
+U16 = mybir.dt.uint16
+U8 = mybir.dt.uint8
+E4M3X4 = mybir.dt.float8_e4m3fn_x4
+E2M1X4 = mybir.dt.float4_e2m1fn_x4
+MULT = mybir.AluOpType.mult
+ADD = mybir.AluOpType.add
+IDENTITY = mybir.ActivationFunctionType.Identity
+
+P = 128
+PASSES = 3
+NT = M // P
+CH = 128
+
+
+def tile_list_heads_bias_kernel(tc, xT, w_words, w_scales, wgt, b, offs, out):
+    nc = tc.nc
+    x_rows = xT.rearrange("(a p i) t -> a i p t", p=P, i=4)
+
+    with ExitStack() as ctx:
+        keep = ctx.enter_context(tc.tile_pool(name="keep", bufs=1))
+        psum = ctx.enter_context(tc.psum_pool(name="psum", bufs=1))
+
+        offsets = keep.tile([P, S // 16], U16, name="offsets")
+        nc.sync.dma_start(offsets[:], offs)
+        weights = keep.tile([P, S], F32, name="weights")
+        nc.scalar.dma_start(out=weights[:, 0:CH], in_=wgt[:, 0:CH])
+
+        warm = keep.tile([P, 1], F32, name="warm")
+        nc.gpsimd.memset(warm[:], 0.0)
+        nc.scalar.activation(out=warm[:], in_=warm[:], func=IDENTITY)
+
+        w_sc = keep.tile([P, PASSES, M], U8, align_bytes=64, name="w_sc")
+        nc.gpsimd.memset(w_sc[:].rearrange("p a n -> p (a n)").bitcast(U32), 0)
+        ident = keep.tile([P, P], F32, name="ident")
+        make_identity(nc, ident[:])
+        b_rows = keep.tile([P, P], F32, name="b_rows")
+        nc.gpsimd.memset(b_rows[:], 0.0)
+
+        x_tiles = []
+        w_codes = keep.tile([P, PASSES, 2 * M], U8, align_bytes=64, name="w_codes")
+        for q in range(4 * PASSES):
+            x_tile = keep.tile([P, T], F32, name="x%d" % q)
+            nc.sync.dma_start(out=x_tile[:], in_=x_rows[q // 4, q % 4])
+            x_tiles.append(x_tile)
+            if q == 0:
+                nc.sync.dma_start(out=weights[:, CH:S], in_=wgt[:, CH:S])
+            if q == 6:
+                nc.sync.dma_start(out=w_codes[:], in_=w_words.rearrange("a p n -> p a n"))
+                for quad in range(4):
+                    nc.sync.dma_start(
+                        out=w_sc[32 * quad:32 * quad + 4, :, :].bitcast(I32),
+                        in_=w_scales.rearrange("a (q r) n -> q r a n", r=4)[quad].bitcast(I32),
+                    )
+                nc.sync.dma_start(out=b_rows[0:NT, :], in_=b.rearrange("(c p) -> c p", p=P))
+
+        codes = keep.tile([P, PASSES, S], U32, align_bytes=64, name="codes")
+        scales = keep.tile([P, PASSES, S], U8, align_bytes=64, name="scales")
+        bank_x = [psum.tile([P, 2 * CH], F32, name="bank_x%d" % m) for m in range(NT)]
+        bias = keep.tile([P, NT], F32, name="bias")
+
+        parts = [(0, 0, 512), (1, 0, 512), (2, 0, 256), (2, 256, 128), (2, 384, 128)]
+        gathered = {}
+        grouped = {}
+        for a, c0, n in parts:
+            gathered[(a, c0)] = keep.tile([P, 4, n], F32, name="g%d_%d" % (a, c0))
+            grouped[(a, c0)] = keep.tile([P, n, 4], BF16, align_bytes=64, name="q%d_%d" % (a, c0))
+
+        def gather(a, c0, i, cuts):
+            for lo, hi in cuts:
+                nc.vector.tensor_tensor(
+                    gathered[(a, c0)][:, i, lo - c0:hi - c0],
+                    x_tiles[4 * a + i][:].indirect(offsets[:, lo // 16:hi // 16]),
+                    weights[:, lo:hi],
+                    MULT,
+                )
+
+        def interleave(a, c0, i0, i1):
+            nc.scalar.copy(
+                out=grouped[(a, c0)][:].rearrange("p (c i) t -> p c t i", i=4)[:, :, i0:i1, :],
+                in_=gathered[(a, c0)][:].rearrange("p t (c i) -> p c t i", i=4)[:, :, i0:i1, :],
+            )
+
+        def quantize(a, c0, n):
+            nc.vector.quantize_mx(
+                out=codes[:, a, c0:c0 + n].bitcast(E4M3X4),
+                scales=scales[:, a, c0:c0 + n],
+                in_=grouped[(a, c0)][:].rearrange("p n t -> p (n t)"),
+            )
+
+        def multiply(a, banks, chunk, m):
+            nc.tensor.matmul_mx(
+                out=banks[m][:, (chunk % 2) * CH:(chunk % 2 + 1) * CH],
+                lhsT=w_codes[:, a, 2 * P * m:2 * P * (m + 1)].bitcast(E2M1X4),
+                lhsT_scale=w_sc[:, a, P * m:P * (m + 1)],
+                rhs=codes[:, a, chunk * CH:(chunk + 1) * CH].bitcast(E4M3X4),
+                rhs_scale=scales[:, a, chunk * CH:(chunk + 1) * CH],
+                start=(a == 0 and chunk % 2 == 0),
+                stop=(a == PASSES - 1 and chunk % 2 == 1),
+            )
+
+        def store(banks, m, pair, on_vector):
+            res = keep.tile([P, 2 * CH], F32, name="res%d_%d" % (m, pair))
+            if on_vector:
+                nc.vector.tensor_scalar(out=res[:], in0=banks[m][:], scalar1=bias[:, m:m + 1], scalar2=None, op0=ADD)
+            else:
+                nc.scalar.activation(out=res[:], in_=banks[m][:], func=IDENTITY, bias=bias[:, m:m + 1])
+            nc.sync.dma_start(out=out[m * P:(m + 1) * P, 2 * CH * pair:2 * CH * (pair + 1)], in_=res[:])
+
+        halves = [(0, 256), (256, 512)]
+        gather(0, 0, 0, [(0, CH), (CH, S)])
+        for i in (1, 2, 3):
+            gather(0, 0, i, halves)
+        interleave(0, 0, 0, 4)
+        for i in (0, 1, 2):
+            gather(1, 0, i, halves)
+        quantize(0, 0, 512)
+        gather(1, 0, 3, halves)
+        interleave(1, 0, 0, 4)
+
+        bias_ps = psum.tile([P, P], F32, name="bias_ps", tag="bank_y3")
+        nc.tensor.transpose(bias_ps[:], b_rows[:], ident[:])
+        nc.scalar.copy(out=bias[:], in_=bias_ps[:, 0:NT])
+        bank_y = [psum.tile([P, 2 * CH], F32, name="bank_y%d" % m) for m in range(NT)]
+
+        for m in range(NT):
+            for c in (0, 1):
+                multiply(0, bank_x, c, m)
+            for c in (2, 3):
+                multiply(0, bank_y, c, m)
+
+        gather(2, 0, 0, [(0, 256)])
+        gather(2, 0, 1, [(0, 256)])
+        interleave(2, 0, 0, 2)
+        gather(2, 0, 2, [(0, 256)])
+        quantize(1, 0, 512)
+        gather(2, 0, 3, [(0, 256)])
+        interleave(2, 0, 2, 4)
+        for m in range(NT):
+            for c in (0, 1):
+                multiply(1, bank_x, c, m)
+        for m in range(NT):
+            for c in (2, 3):
+                multiply(1, bank_y, c, m)
+
+        gather(2, 256, 0, [(256, 384)])
+        gather(2, 256, 1, [(256, 384)])
+        interleave(2, 256, 0, 2)
+        gather(2, 256, 2, [(256, 384)])
+        quantize(2, 0, 256)
+        for m in range(NT):
+            for c in (0, 1):
+                multiply(2, bank_x, c, m)
+        gather(2, 256, 3, [(256, 384)])
+        interleave(2, 256, 2, 4)
+        store(bank_x, 0, 0, False)
+        gather(2, 384, 0, [(384, 512)])
+        gather(2, 384, 1, [(384, 512)])
+        interleave(2, 384, 0, 2)
+        store(bank_x, 1, 0, False)
+        gather(2, 384, 2, [(384, 512)])
+        quantize(2, 256, 128)
+        for m in range(NT):
+            multiply(2, bank_y, 2, m)
+        gather(2, 384, 3, [(384, 512)])
+        interleave(2, 384, 2, 4)
+        quantize(2, 384, 128)
+        store(bank_x, 2, 0, False)
+        store(bank_x, 3, 0, False)
+        for m in range(NT):
+            multiply(2, bank_y, 3, m)
+            store(bank_y, m, 1, m % 2 == 0)

@@ -43,10 +43,10 @@ def tile_list_heads_bias_kernel(tc, xT, w_words, w_scales, wgt, b, offs, out):
 
         w_sc = keep.tile([P, PASSES, M], U8, align_bytes=64, name="w_sc")
         nc.gpsimd.memset(w_sc[:].rearrange("p a n -> p (a n)").bitcast(U32), 0)
-        ident = keep.tile([P, P], F32, name="ident")
-        make_identity(nc, ident[:])
         b_rows = keep.tile([P, P], F32, name="b_rows")
         nc.gpsimd.memset(b_rows[:], 0.0)
+        ident = keep.tile([P, P], F32, name="ident")
+        make_identity(nc, ident[:])
 
         x_tiles = []
         w_codes = keep.tile([P, PASSES, 2 * M], U8, align_bytes=64, name="w_codes")
@@ -74,22 +74,30 @@ def tile_list_heads_bias_kernel(tc, xT, w_words, w_scales, wgt, b, offs, out):
         gathered = {}
         grouped = {}
         for a, c0, n in parts:
-            gathered[(a, c0)] = keep.tile([P, 4, n], F32, name="g%d_%d" % (a, c0))
+            pairs = 2 if c0 == 384 else 1
+            gathered[(a, c0)] = [
+                keep.tile([P, 4 // pairs, n], F32, name="g%d_%d_%d" % (a, c0, k)) for k in range(pairs)
+            ]
             grouped[(a, c0)] = keep.tile([P, n, 4], BF16, align_bytes=64, name="q%d_%d" % (a, c0))
 
         def gather(a, c0, i, cuts):
             for lo, hi in cuts:
+                tiles = gathered[(a, c0)]
+                per = 4 // len(tiles)
                 nc.vector.tensor_tensor(
-                    gathered[(a, c0)][:, i, lo - c0:hi - c0],
+                    tiles[i // per][:, i % per, lo - c0:hi - c0],
                     x_tiles[4 * a + i][:].indirect(offsets[:, lo // 16:hi // 16]),
                     weights[:, lo:hi],
                     MULT,
                 )
 
         def interleave(a, c0, i0, i1):
+            tiles = gathered[(a, c0)]
+            per = 4 // len(tiles)
+            j0 = i0 % per
             nc.scalar.copy(
                 out=grouped[(a, c0)][:].rearrange("p (c i) t -> p c t i", i=4)[:, :, i0:i1, :],
-                in_=gathered[(a, c0)][:].rearrange("p t (c i) -> p c t i", i=4)[:, :, i0:i1, :],
+                in_=tiles[i0 // per][:].rearrange("p t (c i) -> p c t i", i=4)[:, :, j0:j0 + i1 - i0, :],
             )
 
         def quantize(a, c0, n):
@@ -99,24 +107,38 @@ def tile_list_heads_bias_kernel(tc, xT, w_words, w_scales, wgt, b, offs, out):
                 in_=grouped[(a, c0)][:].rearrange("p n t -> p (n t)"),
             )
 
-        def multiply(a, banks, chunk, m):
+        def multiply(a, chunk, m):
+            if chunk < 2:
+                bank, place = bank_x[m], chunk
+            else:
+                bank, place = bank_y[chunk][m // 2], m % 2
             nc.tensor.matmul_mx(
-                out=banks[m][:, (chunk % 2) * CH:(chunk % 2 + 1) * CH],
+                out=bank[:, place * CH:(place + 1) * CH],
                 lhsT=w_codes[:, a, 2 * P * m:2 * P * (m + 1)].bitcast(E2M1X4),
                 lhsT_scale=w_sc[:, a, P * m:P * (m + 1)],
                 rhs=codes[:, a, chunk * CH:(chunk + 1) * CH].bitcast(E4M3X4),
                 rhs_scale=scales[:, a, chunk * CH:(chunk + 1) * CH],
-                start=(a == 0 and chunk % 2 == 0),
-                stop=(a == PASSES - 1 and chunk % 2 == 1),
+                start=(a == 0 and place == 0),
+                stop=(a == PASSES - 1 and place == 1),
             )
 
-        def store(banks, m, pair, on_vector):
-            res = keep.tile([P, 2 * CH], F32, name="res%d_%d" % (m, pair))
+        def add_bias(dst, src, m, on_vector):
             if on_vector:
-                nc.vector.tensor_scalar(out=res[:], in0=banks[m][:], scalar1=bias[:, m:m + 1], scalar2=None, op0=ADD)
+                nc.vector.tensor_scalar(out=dst, in0=src, scalar1=bias[:, m:m + 1], scalar2=None, op0=ADD)
             else:
-                nc.scalar.activation(out=res[:], in_=banks[m][:], func=IDENTITY, bias=bias[:, m:m + 1])
-            nc.sync.dma_start(out=out[m * P:(m + 1) * P, 2 * CH * pair:2 * CH * (pair + 1)], in_=res[:])
+                nc.scalar.activation(out=dst, in_=src, func=IDENTITY, bias=bias[:, m:m + 1])
+
+        def finish_x(res, m, on_vector):
+            add_bias(res, bank_x[m][:], m, on_vector)
+            nc.sync.dma_start(out=out[m * P:(m + 1) * P, 0:2 * CH], in_=res)
+
+        def finish_y(res, chunk, h, on_vector):
+            for k in (0, 1):
+                add_bias(res[:, k, :], bank_y[chunk][h][:, k * CH:(k + 1) * CH], 2 * h + k, on_vector)
+            nc.sync.dma_start(
+                out=out[2 * h * P:2 * (h + 1) * P, chunk * CH:(chunk + 1) * CH].rearrange("(k p) j -> p k j", p=P),
+                in_=res,
+            )
 
         halves = [(0, 256), (256, 512)]
         gather(0, 0, 0, [(0, CH), (CH, S)])
@@ -129,16 +151,16 @@ def tile_list_heads_bias_kernel(tc, xT, w_words, w_scales, wgt, b, offs, out):
         gather(1, 0, 3, halves)
         interleave(1, 0, 0, 4)
 
-        bias_ps = psum.tile([P, P], F32, name="bias_ps", tag="bank_y3")
+        bias_ps = psum.tile([P, P], F32, name="bias_ps", tag="bank_y3_1")
         nc.tensor.transpose(bias_ps[:], b_rows[:], ident[:])
         nc.scalar.copy(out=bias[:], in_=bias_ps[:, 0:NT])
-        bank_y = [psum.tile([P, 2 * CH], F32, name="bank_y%d" % m) for m in range(NT)]
+        bank_y = {}
+        for c in (2, 3):
+            bank_y[c] = [psum.tile([P, 2 * CH], F32, name="bank_y%d_%d" % (c, h)) for h in (0, 1)]
 
-        for m in range(NT):
-            for c in (0, 1):
-                multiply(0, bank_x, c, m)
-            for c in (2, 3):
-                multiply(0, bank_y, c, m)
+        for c in range(4):
+            for m in range(NT):
+                multiply(0, c, m)
 
         gather(2, 0, 0, [(0, 256)])
         gather(2, 0, 1, [(0, 256)])
@@ -147,12 +169,9 @@ def tile_list_heads_bias_kernel(tc, xT, w_words, w_scales, wgt, b, offs, out):
         quantize(1, 0, 512)
         gather(2, 0, 3, [(0, 256)])
         interleave(2, 0, 2, 4)
-        for m in range(NT):
-            for c in (0, 1):
-                multiply(1, bank_x, c, m)
-        for m in range(NT):
-            for c in (2, 3):
-                multiply(1, bank_y, c, m)
+        for c in range(4):
+            for m in range(NT):
+                multiply(1, c, m)
 
         gather(2, 256, 0, [(256, 384)])
         gather(2, 256, 1, [(256, 384)])
@@ -161,23 +180,30 @@ def tile_list_heads_bias_kernel(tc, xT, w_words, w_scales, wgt, b, offs, out):
         quantize(2, 0, 256)
         for m in range(NT):
             for c in (0, 1):
-                multiply(2, bank_x, c, m)
+                multiply(2, c, m)
         gather(2, 256, 3, [(256, 384)])
         interleave(2, 256, 2, 4)
-        store(bank_x, 0, 0, False)
         gather(2, 384, 0, [(384, 512)])
         gather(2, 384, 1, [(384, 512)])
         interleave(2, 384, 0, 2)
-        store(bank_x, 1, 0, False)
         gather(2, 384, 2, [(384, 512)])
         quantize(2, 256, 128)
         for m in range(NT):
-            multiply(2, bank_y, 2, m)
+            multiply(2, 2, m)
         gather(2, 384, 3, [(384, 512)])
         interleave(2, 384, 2, 4)
         quantize(2, 384, 128)
-        store(bank_x, 2, 0, False)
-        store(bank_x, 3, 0, False)
         for m in range(NT):
-            multiply(2, bank_y, 3, m)
-            store(bank_y, m, 1, m % 2 == 0)
+            multiply(2, 3, m)
+
+        res_a = keep.tile([P, 2, 2 * CH], F32, name="res_a", tag="g2_384_0")
+        for m in (0, 1):
+            finish_x(res_a[:, m, :], m, True)
+        res_b = keep.tile([P, 8, CH], F32, name="res_b", tag="g2_384_1")
+        for m in (2, 3):
+            finish_x(res_b[:, 2 * m - 4:2 * m - 2, :].rearrange("p k j -> p (k j)"), m, False)
+        finish_y(res_b[:, 4:6, :], 2, 0, True)
+        finish_y(res_b[:, 6:8, :], 2, 1, False)
+        res_c = keep.tile([P, 4, CH], F32, name="res_c")
+        finish_y(res_c[:, 0:2, :], 3, 0, True)
+        finish_y(res_c[:, 2:4, :], 3, 1, False)

from contextlib import ExitStack

import concourse.mybir as mybir
from concourse.masks import make_identity

K, M, T, S = 1536, 512, 1024, 512
FLOPS = 2 * K * M * S

F32 = mybir.dt.float32
BF16 = mybir.dt.bfloat16
I32 = mybir.dt.int32
U32 = mybir.dt.uint32
U16 = mybir.dt.uint16
U8 = mybir.dt.uint8
E4M3X4 = mybir.dt.float8_e4m3fn_x4
E2M1X4 = mybir.dt.float4_e2m1fn_x4
MULT = mybir.AluOpType.mult
ADD = mybir.AluOpType.add
IDENTITY = mybir.ActivationFunctionType.Identity

P = 128
PASSES = 3
NT = M // P
CH = 128


def tile_list_heads_bias_kernel(tc, xT, w_words, w_scales, wgt, b, offs, out):
    nc = tc.nc
    x_rows = xT.rearrange("(a p i) t -> a i p t", p=P, i=4)

    with ExitStack() as ctx:
        keep = ctx.enter_context(tc.tile_pool(name="keep", bufs=1))
        psum = ctx.enter_context(tc.psum_pool(name="psum", bufs=1))

        offsets = keep.tile([P, S // 16], U16, name="offsets")
        nc.sync.dma_start(offsets[:], offs)
        weights = keep.tile([P, S], F32, name="weights")
        nc.scalar.dma_start(out=weights[:, 0:CH], in_=wgt[:, 0:CH])

        warm = keep.tile([P, 1], F32, name="warm")
        nc.gpsimd.memset(warm[:], 0.0)
        nc.scalar.activation(out=warm[:], in_=warm[:], func=IDENTITY)

        w_sc = keep.tile([P, PASSES, M], U8, align_bytes=64, name="w_sc")
        nc.gpsimd.memset(w_sc[:].rearrange("p a n -> p (a n)").bitcast(U32), 0)
        b_rows = keep.tile([P, P], F32, name="b_rows")
        nc.gpsimd.memset(b_rows[:], 0.0)
        ident = keep.tile([P, P], F32, name="ident")
        make_identity(nc, ident[:])

        x_tiles = []
        w_codes = keep.tile([P, PASSES, 2 * M], U8, align_bytes=64, name="w_codes")
        for q in range(4 * PASSES):
            x_tile = keep.tile([P, T], F32, name="x%d" % q)
            nc.sync.dma_start(out=x_tile[:], in_=x_rows[q // 4, q % 4])
            x_tiles.append(x_tile)
            if q == 0:
                nc.sync.dma_start(out=weights[:, CH:S], in_=wgt[:, CH:S])
            if q == 6:
                nc.sync.dma_start(out=w_codes[:], in_=w_words.rearrange("a p n -> p a n"))
                for quad in range(4):
                    nc.sync.dma_start(
                        out=w_sc[32 * quad:32 * quad + 4, :, :].bitcast(I32),
                        in_=w_scales.rearrange("a (q r) n -> q r a n", r=4)[quad].bitcast(I32),
                    )
                nc.sync.dma_start(out=b_rows[0:NT, :], in_=b.rearrange("(c p) -> c p", p=P))

        codes = keep.tile([P, PASSES, S], U32, align_bytes=64, name="codes")
        scales = keep.tile([P, PASSES, S], U8, align_bytes=64, name="scales")
        bank_x = [psum.tile([P, 2 * CH], F32, name="bank_x%d" % m) for m in range(NT)]
        bias = keep.tile([P, NT], F32, name="bias")

        parts = [(0, 0, 512), (1, 0, 512), (2, 0, 256), (2, 256, 128), (2, 384, 128)]
        gathered = {}
        grouped = {}
        for a, c0, n in parts:
            pairs = 2 if c0 == 384 else 1
            gathered[(a, c0)] = [
                keep.tile([P, 4 // pairs, n], F32, name="g%d_%d_%d" % (a, c0, k)) for k in range(pairs)
            ]
            grouped[(a, c0)] = keep.tile([P, n, 4], BF16, align_bytes=64, name="q%d_%d" % (a, c0))

        def gather(a, c0, i, cuts):
            for lo, hi in cuts:
                tiles = gathered[(a, c0)]
                per = 4 // len(tiles)
                nc.vector.tensor_tensor(
                    tiles[i // per][:, i % per, lo - c0:hi - c0],
                    x_tiles[4 * a + i][:].indirect(offsets[:, lo // 16:hi // 16]),
                    weights[:, lo:hi],
                    MULT,
                )

        def interleave(a, c0, i0, i1):
            tiles = gathered[(a, c0)]
            per = 4 // len(tiles)
            j0 = i0 % per
            nc.scalar.copy(
                out=grouped[(a, c0)][:].rearrange("p (c i) t -> p c t i", i=4)[:, :, i0:i1, :],
                in_=tiles[i0 // per][:].rearrange("p t (c i) -> p c t i", i=4)[:, :, j0:j0 + i1 - i0, :],
            )

        def quantize(a, c0, n):
            nc.vector.quantize_mx(
                out=codes[:, a, c0:c0 + n].bitcast(E4M3X4),
                scales=scales[:, a, c0:c0 + n],
                in_=grouped[(a, c0)][:].rearrange("p n t -> p (n t)"),
            )

        def multiply(a, chunk, m):
            if chunk < 2:
                bank, place = bank_x[m], chunk
            else:
                bank, place = bank_y[chunk][m // 2], m % 2
            nc.tensor.matmul_mx(
                out=bank[:, place * CH:(place + 1) * CH],
                lhsT=w_codes[:, a, 2 * P * m:2 * P * (m + 1)].bitcast(E2M1X4),
                lhsT_scale=w_sc[:, a, P * m:P * (m + 1)],
                rhs=codes[:, a, chunk * CH:(chunk + 1) * CH].bitcast(E4M3X4),
                rhs_scale=scales[:, a, chunk * CH:(chunk + 1) * CH],
                start=(a == 0 and place == 0),
                stop=(a == PASSES - 1 and place == 1),
            )

        def add_bias(dst, src, m, on_vector):
            if on_vector:
                nc.vector.tensor_scalar(out=dst, in0=src, scalar1=bias[:, m:m + 1], scalar2=None, op0=ADD)
            else:
                nc.scalar.activation(out=dst, in_=src, func=IDENTITY, bias=bias[:, m:m + 1])

        def finish_x(res, m, on_vector):
            add_bias(res, bank_x[m][:], m, on_vector)
            nc.sync.dma_start(out=out[m * P:(m + 1) * P, 0:2 * CH], in_=res)

        def finish_y(res, chunk, h, on_vector):
            for k in (0, 1):
                add_bias(res[:, k, :], bank_y[chunk][h][:, k * CH:(k + 1) * CH], 2 * h + k, on_vector)
            nc.sync.dma_start(
                out=out[2 * h * P:2 * (h + 1) * P, chunk * CH:(chunk + 1) * CH].rearrange("(k p) j -> p k j", p=P),
                in_=res,
            )

        halves = [(0, 256), (256, 512)]
        gather(0, 0, 0, [(0, CH), (CH, S)])
        for i in (1, 2, 3):
            gather(0, 0, i, halves)
        interleave(0, 0, 0, 4)
        for i in (0, 1, 2):
            gather(1, 0, i, halves)
        quantize(0, 0, 512)
        gather(1, 0, 3, halves)
        interleave(1, 0, 0, 4)

        bias_ps = psum.tile([P, P], F32, name="bias_ps", tag="bank_y3_1")
        nc.tensor.transpose(bias_ps[:], b_rows[:], ident[:])
        nc.scalar.copy(out=bias[:], in_=bias_ps[:, 0:NT])
        bank_y = {}
        for c in (2, 3):
            bank_y[c] = [psum.tile([P, 2 * CH], F32, name="bank_y%d_%d" % (c, h)) for h in (0, 1)]

        for c in range(4):
            for m in range(NT):
                multiply(0, c, m)

        gather(2, 0, 0, [(0, 256)])
        gather(2, 0, 1, [(0, 256)])
        interleave(2, 0, 0, 2)
        gather(2, 0, 2, [(0, 256)])
        quantize(1, 0, 512)
        gather(2, 0, 3, [(0, 256)])
        interleave(2, 0, 2, 4)
        for c in range(4):
            for m in range(NT):
                multiply(1, c, m)

        gather(2, 256, 0, [(256, 384)])
        gather(2, 256, 1, [(256, 384)])
        interleave(2, 256, 0, 2)
        gather(2, 256, 2, [(256, 384)])
        quantize(2, 0, 256)
        for m in range(NT):
            for c in (0, 1):
                multiply(2, c, m)
        gather(2, 256, 3, [(256, 384)])
        interleave(2, 256, 2, 4)
        gather(2, 384, 0, [(384, 512)])
        gather(2, 384, 1, [(384, 512)])
        interleave(2, 384, 0, 2)
        gather(2, 384, 2, [(384, 512)])
        quantize(2, 256, 128)
        for m in range(NT):
            multiply(2, 2, m)
        gather(2, 384, 3, [(384, 512)])
        interleave(2, 384, 2, 4)
        quantize(2, 384, 128)
        for m in range(NT):
            multiply(2, 3, m)

        res_a = keep.tile([P, 2, 2 * CH], F32, name="res_a", tag="g2_384_0")
        for m in (0, 1):
            finish_x(res_a[:, m, :], m, True)
        res_b = keep.tile([P, 8, CH], F32, name="res_b", tag="g2_384_1")
        for m in (2, 3):
            finish_x(res_b[:, 2 * m - 4:2 * m - 2, :].rearrange("p k j -> p (k j)"), m, False)
        finish_y(res_b[:, 4:6, :], 2, 0, True)
        finish_y(res_b[:, 6:8, :], 2, 1, False)
        res_c = keep.tile([P, 4, CH], F32, name="res_c")
        finish_y(res_c[:, 0:2, :], 3, 0, True)
        finish_y(res_c[:, 2:4, :], 3, 1, False)
